import numpy as np
import ml_dtypes


def mxq(x, axis, fmt="e4m3"):
    dtype, down = {"e4m3": (ml_dtypes.float8_e4m3fn, 7), "e5m2": (ml_dtypes.float8_e5m2, 14)}[fmt]
    v = np.moveaxis(np.asarray(x, np.float32).astype(ml_dtypes.bfloat16).astype(np.float64), axis, -1)
    blocks = v.reshape(v.shape[:-1] + (-1, 32))
    amax = np.abs(blocks).max(-1, keepdims=True)
    byte = np.maximum(np.where(amax > 0, np.frexp(amax)[1] - 1 + 127, 0) - down, 1)
    scale = np.exp2(byte - 127.0)
    codes = (blocks / scale).astype(np.float32).astype(dtype).astype(np.float64)
    return np.moveaxis((codes * scale).reshape(v.shape), -1, axis)


WIDE = False


def mx_kscale(k):
    if not WIDE:
        return np.ones(k)
    levels = np.array([10, -10, 5, -5, 0])
    if k % 512:
        return np.exp2(np.random.permutation(np.resize(levels, k // 32))).repeat(32)
    a = np.empty((k // 512, 16))
    for p in range(k // 512):
        a[p, :8] = np.random.permutation(np.resize(levels, 8))
        for g in range(8):
            far = levels[np.abs(levels - a[p, g]) >= 10]
            a[p, g + 8] = far[np.random.randint(len(far))]
    return np.exp2(a.ravel()).repeat(32)


def f64(x):
    return np.asarray(x).astype(np.float64)


def striped(idx):
    return np.tile(idx.reshape(-1, 16).T, (8, 1)).astype(np.uint16)


def unstriped(offs):
    return offs[:16].T.reshape(-1).astype(np.int64)


def striped8(idx):
    return np.concatenate([x.reshape(-1, 16).T for x in idx]).astype(np.uint16)


def runs(offs, k):
    lists = np.stack([offs[16 * r : 16 * r + 16].T.reshape(-1) for r in range(8)]).astype(np.int64)
    return lists[np.arange(k) % 512 // 64]


def pack_weight(w):
    k, n = w.shape
    w = f64(np.asarray(w, np.float32).astype(ml_dtypes.bfloat16)).reshape(k // 32, 32, n)
    amax = np.abs(w).max(1)
    byte = np.clip(np.where(amax > 0, np.frexp(amax)[1] - 1 + 127 - 7, 1), 1, 254)
    scaled = (w * np.exp2(127.0 - byte)[:, None, :]).reshape(k, n).astype(np.float32)
    words = np.ascontiguousarray(scaled.reshape(k // 512, 128, 4, n).transpose(0, 1, 3, 2)).astype(ml_dtypes.float8_e4m3fn).view(np.uint8)
    return words, np.ascontiguousarray(byte.astype(np.uint8).reshape(k // 512, 16, n))


def unpack_weight(words, scales):
    g, p, n, _ = words.shape
    vals = np.ascontiguousarray(words).view(ml_dtypes.float8_e4m3fn).astype(np.float64) * np.repeat(np.exp2(scales.astype(np.float64) - 127.0), 8, axis=1)[..., None]
    return vals.transpose(0, 1, 3, 2).reshape(g * 512, n)


def sigmoid(v):
    return 1.0 / (1.0 + np.exp(-np.maximum(v, -700.0)))


K, T, S, N, H = 512, 2048, 512, 512, 512


def setup_inputs():
    n = np.random.standard_normal
    s = mx_kscale(K)[:, None]
    u = mx_kscale(H)
    packed_xT = pack_weight(n((K, T)) * s)
    return {
        "x_words": packed_xT[0],
        "x_scales": packed_xT[1],
        "w1": (n((K, H)) / np.sqrt(K) / s).astype(np.float32),
        "gn": (np.random.uniform(0.5, 1.5, (H, 1)) * u[:, None]).astype(np.float32),
        "w2": (n((H, N)) / np.sqrt(H) / u[:, None]).astype(np.float32),
        "offs": striped(np.random.permutation(T)[:S]),
        "n1": striped8(np.stack([np.random.permutation(S) for _ in range(8)])),
        "n2": striped8(np.stack([np.random.permutation(S) for _ in range(8)])),
        "n3": striped8(np.stack([np.random.permutation(S) for _ in range(8)])),
        "n4": striped8(np.stack([np.random.permutation(S) for _ in range(8)])),
    }


def reference(x_words, x_scales, w1, gn, w2, offs, n1, n2, n3, n4):
    xq = unpack_weight(x_words, x_scales)[:, unstriped(offs)]
    y = mxq(f64(w1), 0, "e4m3").T @ xq
    st = y[np.arange(H)[:, None], runs(n1, H)] - y
    z = f64(gn) * (y * (sigmoid(st[np.arange(H)[:, None], runs(n2, H)])))
    h = mxq(f64(w2), 0, "e4m3").T @ mxq(z, 0, "e4m3")
    return h - (np.minimum(h[np.arange(N)[:, None], runs(n3, N)], h[np.arange(N)[:, None], runs(n4, N)]))

@@ -1,0 +1,188 @@
+from contextlib import ExitStack
+
+import concourse.mybir as mybir
+
+K, T, S, N, H = 512, 2048, 512, 512, 512
+FLOPS = 2 * K * H * S + 2 * H * N * S
+
+F32 = mybir.dt.float32
+BF16 = mybir.dt.bfloat16
+I32 = mybir.dt.int32
+U32 = mybir.dt.uint32
+U16 = mybir.dt.uint16
+U8 = mybir.dt.uint8
+FP8X4 = mybir.dt.float8_e4m3fn_x4
+ALU = mybir.AluOpType
+ACT = mybir.ActivationFunctionType
+
+P = 128
+PACK = 4
+HALF = S // 2
+LC = HALF // 16
+PIECES = [(0, 256), (256, 256)]
+
+
+def tile_picked_layhopdunder_none_p_kernel(
+    tc, x_words, x_scales, w1, gn, w2, offs, n1, n2, n3, n4, out
+):
+    nc = tc.nc
+    halves = range(2)
+    tiles = range(PACK)
+
+    def cols(u):
+        return slice(u * HALF, (u + 1) * HALF)
+
+    def entries(lst, u):
+        return lst[:, u * LC : (u + 1) * LC]
+
+    with ExitStack() as ctx:
+        sb = ctx.enter_context(tc.tile_pool(name="sb", bufs=1))
+        ps = ctx.enter_context(tc.psum_pool(name="ps", bufs=1))
+
+        def new(shape, dtype, name, tag=None):
+            return sb.tile(shape, dtype, name=name, tag=tag or name, align_bytes=64)
+
+        lists = {}
+        for name in ("offs", "n1", "n2", "n3", "n4"):
+            lists[name] = new([P, S // 16], U16, name)
+        w1_raw = new([P, PACK, H], F32, "w_raw")
+        xw = new([P, T], I32, "xw")
+        xs = new([P, T], U8, "xs")
+        gain = new([P, PACK], F32, "gain")
+
+        xs_words = xs[:].bitcast(I32)
+        nc.vector.memset(xs_words, 0)
+        for name, source in (("offs", offs), ("n1", n1), ("n2", n2), ("n3", n3)):
+            nc.sync.dma_start(lists[name][:], source)
+        nc.sync.dma_start(w1_raw[:], w1.rearrange("(p j) c -> p j c", j=PACK))
+        nc.sync.dma_start(xw[:], x_words[0].rearrange("p n t -> p (n t)").bitcast(I32))
+        nc.sync.dma_start(lists["n4"][:], n4)
+        nc.sync.dma_start(gain[:], gn.rearrange("(p t) o -> p (t o)", t=PACK))
+        for q in range(4):
+            nc.scalar.dma_start(
+                xs_words[32 * q : 32 * q + 4, :],
+                x_scales[0, 4 * q : 4 * q + 4, :].bitcast(I32),
+            )
+
+        def deal_views(dealt, raw):
+            return (
+                dealt[:].rearrange("p (t m j) -> p m j t", t=PACK, j=PACK),
+                raw[:].rearrange("p j (m t) -> p m j t", t=PACK),
+            )
+
+        def quantise(values, name, width, codes_tag=None):
+            codes = new([P, width], U32, name + "_codes", codes_tag)
+            scales = new([P, width], U8, name + "_scales")
+            nc.vector.quantize_mx(out=codes[:].bitcast(FP8X4), scales=scales[:], in_=values)
+            return codes, scales
+
+        def product(bank, w, t, moving_codes, moving_scales):
+            m = slice(t * P, (t + 1) * P)
+            nc.tensor.matmul_mx(
+                out=bank,
+                lhsT=w[0][:, m].bitcast(FP8X4),
+                lhsT_scale=w[1][:, m],
+                rhs=moving_codes.bitcast(FP8X4),
+                rhs_scale=moving_scales,
+                start=True,
+                stop=True,
+            )
+
+        xs_g = new([P, S], U8, "xs_g")
+        nc.vector.tensor_copy(xs_g[:], xs[:].indirect(lists["offs"][:]))
+        w1_bf = new([P, PACK * H], BF16, "w1_bf")
+        dst, src = deal_views(w1_bf, w1_raw)
+        nc.vector.tensor_copy(dst[:, :48], src[:, :48])
+        nc.scalar.copy(dst[:, 48:], src[:, 48:])
+        w2_raw = new([P, PACK, N], F32, "w_raw")
+        nc.sync.dma_start(w2_raw[:], w2.rearrange("(p j) c -> p j c", j=PACK))
+        w1_q = quantise(w1_bf[:], "w1", H, "xs")
+
+        y_ps = [ps.tile([P, S], F32, name=f"y_ps{t}", tag=f"low_bank{t}") for t in tiles]
+        xw_g = new([P, S], U32, "xw_g", "w1_bf")
+        for u in halves:
+            nc.vector.tensor_copy(xw_g[:, cols(u)], xw[:].bitcast(U32).indirect(entries(lists["offs"], u)))
+        for pair in (0, 2):
+            for u in halves:
+                for t in (pair, pair + 1):
+                    product(y_ps[t][:, cols(u)], w1_q, t, xw_g[:, cols(u)], xs_g[:, cols(u)])
+
+        def gather(on_vector, dst_ap, window, lst, u):
+            looked_up = window[:].indirect(entries(lists[lst], u))
+            if on_vector:
+                nc.vector.tensor_copy(dst_ap, looked_up)
+            else:
+                nc.scalar.activation(dst_ap, looked_up, ACT.Copy)
+
+        y = [new([P, S], F32, f"y{t}") for t in tiles]
+        hop = [new([P, S], F32, f"hop{t}") for t in tiles]
+        st = [new([P, S], F32, f"st{t}") for t in tiles]
+        for t in tiles:
+            if t in (0,):
+                nc.vector.tensor_copy(y[t][:], y_ps[t][:])
+            else:
+                nc.scalar.copy(y[t][:], y_ps[t][:])
+        for t in tiles:
+            for u in halves:
+                gather((t, u) not in ((1, 0), (1, 1), (3, 0), (3, 1)), hop[t][:, cols(u)], y[t], "n1", u)
+        for t in tiles:
+            nc.vector.tensor_tensor(st[t][:], hop[t][:], y_ps[t][:], ALU.subtract)
+
+        h_ps = [ps.tile([P, S], F32, name=f"h_ps{t}", tag=f"high_bank{t}") for t in tiles]
+        h = [new([P, S], F32, f"h{t}") for t in tiles]
+        w2_q = None
+        gates = [new([P, HALF], F32, f"gate{r}") for r in range(4)]
+        last = len(PIECES) - 1
+        for u, (c0, width) in enumerate(PIECES):
+            c = slice(c0, c0 + width)
+            z = new([P, PACK, width], BF16, f"z{u}")
+            for t in tiles:
+                gate = gates[(u * PACK + t) % len(gates)][:, :width]
+                looked_up = st[t][:].indirect(lists["n2"][:, c0 // 16 : (c0 + width) // 16])
+                nc.scalar.activation(gate, looked_up, ACT.Sigmoid)
+                nc.vector.scalar_tensor_tensor(
+                    z[:, t, :], y_ps[t][:, c], gain[:, t : t + 1], gate, ALU.mult, ALU.mult
+                )
+            if u == 0:
+                w2_bf = new([P, PACK * N], BF16, "w2_bf")
+                dst, src = deal_views(w2_bf, w2_raw)
+                for m0 in range(0, P, 32):
+                    if m0 < 128:
+                        nc.vector.tensor_copy(dst[:, m0 : m0 + 32], src[:, m0 : m0 + 32])
+                    else:
+                        nc.scalar.copy(dst[:, m0 : m0 + 32], src[:, m0 : m0 + 32])
+                w2_q = quantise(w2_bf[:], "w2", N)
+            zi = new([P, PACK * width], BF16, f"zi{u}")
+            nc.vector.tensor_copy(
+                zi[:].rearrange("p (c i t) -> p c t i", i=4, t=PACK),
+                z[:].rearrange("p t (c i) -> p c t i", i=4),
+            )
+            z_q = quantise(zi[:], f"z{u}", width)
+            if u == last:
+                for t in tiles:
+                    nc.scalar.copy(h[t][:, :c0], h_ps[t][:, :c0])
+                tail_ps = [ps.tile([P, S], F32, name=f"tail_ps{t}", tag=f"low_bank{t}") for t in tiles]
+            for t in tiles:
+                bank = tail_ps[t] if u == last else h_ps[t]
+                product(bank[:, c], w2_q, t, z_q[0][:], z_q[1][:])
+
+        out_rows = out.rearrange("(p t) n -> p t n", t=PACK)
+        for t in tiles:
+            if t in (1,3):
+                nc.vector.tensor_copy(h[t][:, c], tail_ps[t][:, c])
+            else:
+                nc.scalar.copy(h[t][:, c], tail_ps[t][:, c])
+        for t in tiles:
+            a = new([P, S], F32, f"a{t}")
+            b = new([P, S], F32, f"b{t}")
+            low = new([P, S], F32, f"low{t}")
+            res = new([P, S], F32, f"res{t}")
+            for u in halves:
+                gather((t, u) in (), a[:, cols(u)], h[t], "n3", u)
+                gather((t, u) not in ((1,1),(2,1),(3,1)), b[:, cols(u)], h[t], "n4", u)
+            pieces = [cols(0), cols(1)] if t == PACK - 1 else [slice(0, S)]
+            for c in pieces:
+                nc.vector.tensor_tensor(low[:, c], a[:, c], b[:, c], ALU.min)
+            for c in pieces:
+                nc.vector.tensor_tensor(res[:, c], h[t][:, c], low[:, c], ALU.subtract)
+                nc.sync.dma_start(out_rows[:, t, c], res[:, c])

@@ -88,6 +88,11 @@ def tile_picked_layhopdunder_none_p_kernel(
                 stop=True,
             )
 
+        warm_in = new([P, 1], F32, "warm_in")
+        warm_out = new([P, 1], F32, "warm_out")
+        nc.vector.memset(warm_in[:], 0.0)
+        nc.scalar.activation(warm_out[:], warm_in[:], ACT.Sigmoid)
+
         xs_g = new([P, S], U8, "xs_g")
         nc.vector.tensor_copy(xs_g[:], xs[:].indirect(lists["offs"][:]))
         w1_bf = new([P, PACK * H], BF16, "w1_bf")

@@ -64,11 +64,10 @@ def tile_picked_layhopdunder_none_p_kernel(
                 x_scales[0, 4 * q : 4 * q + 4, :].bitcast(I32),
             )
 
-        def deal_views(dealt, raw):
-            return (
-                dealt[:].rearrange("p (t m j) -> p m j t", t=PACK, j=PACK),
-                raw[:].rearrange("p j (m t) -> p m j t", t=PACK),
-            )
+        def pair_views(dealt, raw, pair):
+            dst = dealt[:].rearrange("p (t m j) -> p m j t", t=2, j=PACK)
+            src = raw[:].rearrange("p j (m t) -> p m j t", t=PACK)[:, :, :, 2 * pair : 2 * pair + 2]
+            return dst, src
 
         def quantise(values, name, width, codes_tag=None):
             codes = new([P, width], U32, name + "_codes", codes_tag)
@@ -95,22 +94,23 @@ def tile_picked_layhopdunder_none_p_kernel(
 
         xs_g = new([P, S], U8, "xs_g")
         nc.vector.tensor_copy(xs_g[:], xs[:].indirect(lists["offs"][:]))
-        w1_bf = new([P, PACK * H], BF16, "w1_bf")
-        dst, src = deal_views(w1_bf, w1_raw)
-        nc.vector.tensor_copy(dst[:, :48], src[:, :48])
-        nc.scalar.copy(dst[:, 48:], src[:, 48:])
+        w1_bf = [new([P, 2 * H], BF16, f"w1_bf{pair}") for pair in range(2)]
+        for pair in range(2):
+            nc.scalar.copy(*pair_views(w1_bf[pair], w1_raw, pair))
         w2_raw = new([P, PACK, N], F32, "w_raw")
         nc.sync.dma_start(w2_raw[:], w2.rearrange("(p j) c -> p j c", j=PACK))
-        w1_q = quantise(w1_bf[:], "w1", H, "xs")
 
         y_ps = [ps.tile([P, S], F32, name=f"y_ps{t}", tag=f"low_bank{t}") for t in tiles]
-        xw_g = new([P, S], U32, "xw_g", "w1_bf")
+        w1_low_q = quantise(w1_bf[0][:], "w1_low", H // 2, "xs")
+        xw_g = new([P, S], U32, "xw_g", "w1_bf0")
         for u in halves:
             nc.vector.tensor_copy(xw_g[:, cols(u)], xw[:].bitcast(U32).indirect(entries(lists["offs"], u)))
-        for pair in (0, 2):
-            for u in halves:
-                for t in (pair, pair + 1):
-                    product(y_ps[t][:, cols(u)], w1_q, t, xw_g[:, cols(u)], xs_g[:, cols(u)])
+        for u in halves:
+            for t in (0, 1):
+                product(y_ps[t][:, cols(u)], w1_low_q, t, xw_g[:, cols(u)], xs_g[:, cols(u)])
+        w1_high_q = quantise(w1_bf[1][:], "w1_high", H // 2, "xw")
+        for t in (2, 3):
+            product(y_ps[t][:], w1_high_q, t - 2, xw_g[:], xs_g[:])
 
         def gather(on_vector, dst_ap, window, lst, u):
             looked_up = window[:].indirect(entries(lists[lst], u))
@@ -135,59 +135,76 @@ def tile_picked_layhopdunder_none_p_kernel(
 
         h_ps = [ps.tile([P, S], F32, name=f"h_ps{t}", tag=f"high_bank{t}") for t in tiles]
         h = [new([P, S], F32, f"h{t}") for t in tiles]
-        w2_q = None
-        gates = [new([P, HALF], F32, f"gate{r}") for r in range(4)]
-        last = len(PIECES) - 1
-        for u, (c0, width) in enumerate(PIECES):
-            c = slice(c0, c0 + width)
-            z = new([P, PACK, width], BF16, f"z{u}")
-            for t in tiles:
-                gate = gates[(u * PACK + t) % len(gates)][:, :width]
-                looked_up = st[t][:].indirect(lists["n2"][:, c0 // 16 : (c0 + width) // 16])
-                nc.scalar.activation(gate, looked_up, ACT.Sigmoid)
-                nc.vector.scalar_tensor_tensor(
-                    z[:, t, :], y_ps[t][:, c], gain[:, t : t + 1], gate, ALU.mult, ALU.mult
-                )
-            if u == 0:
-                w2_bf = new([P, PACK * N], BF16, "w2_bf")
-                dst, src = deal_views(w2_bf, w2_raw)
-                for m0 in range(0, P, 32):
-                    if m0 < 128:
-                        nc.vector.tensor_copy(dst[:, m0 : m0 + 32], src[:, m0 : m0 + 32])
-                    else:
-                        nc.scalar.copy(dst[:, m0 : m0 + 32], src[:, m0 : m0 + 32])
-                w2_q = quantise(w2_bf[:], "w2", N)
-            zi = new([P, PACK * width], BF16, f"zi{u}")
+        gates = [new([P, HALF], F32, f"gate{r}") for r in tiles]
+        def gate_and_scale(z, t, c0, width, z0):
+            looked_up = st[t][:].indirect(lists["n2"][:, c0 // 16 : (c0 + width) // 16])
+            gate = gates[t][:, z0 : z0 + width]
+            nc.scalar.activation(gate, looked_up, ACT.Sigmoid)
+            nc.vector.scalar_tensor_tensor(
+                z[:, t, z0 : z0 + width], y_ps[t][:, c0 : c0 + width], gain[:, t : t + 1], gate, ALU.mult, ALU.mult
+            )
+
+        def weave_and_quantise(z, name, z0, width):
+            zi = new([P, PACK * width], BF16, name + "_woven")
             nc.vector.tensor_copy(
                 zi[:].rearrange("p (c i t) -> p c t i", i=4, t=PACK),
-                z[:].rearrange("p t (c i) -> p c t i", i=4),
+                z[:, :, z0 : z0 + width].rearrange("p t (c i) -> p c t i", i=4),
             )
-            z_q = quantise(zi[:], f"z{u}", width)
-            if u == last:
-                for t in tiles:
-                    nc.scalar.copy(h[t][:, :c0], h_ps[t][:, :c0])
-                tail_ps = [ps.tile([P, S], F32, name=f"tail_ps{t}", tag=f"low_bank{t}") for t in tiles]
-            for t in tiles:
-                bank = tail_ps[t] if u == last else h_ps[t]
-                product(bank[:, c], w2_q, t, z_q[0][:], z_q[1][:])
+            return quantise(zi[:], name, width)
+
+        z_q = []
+        z = new([P, PACK, HALF], BF16, "z0")
+        for t in tiles:
+            gate_and_scale(z, t, 0, HALF, 0)
+        w2_low = new([P, 2 * N], BF16, "w2_low")
+        for t in (0, 1):
+            dst, src = [view[:, :, :, t] for view in pair_views(w2_low, w2_raw, 0)]
+            nc.gpsimd.tensor_scalar(dst, src, 1.0, 0.0, ALU.mult, ALU.add)
+        low_q = quantise(w2_low[:], "w2_low", N // 2)
+        z_q.append((0, HALF, weave_and_quantise(z, "zq0", 0, HALF)))
+        for t in (0, 1):
+            product(h_ps[t][:, cols(0)], low_q, t, z_q[0][2][0][:], z_q[0][2][1][:])
+            nc.scalar.copy(h[t][:, cols(0)], h_ps[t][:, cols(0)])
+        z = new([P, PACK, HALF], BF16, "z1")
+        for t in range(PACK - 1):
+            gate_and_scale(z, t, HALF, HALF, 0)
+        tail_ps = [ps.tile([P, HALF], F32, name=f"tail_ps{t}", tag=f"low_bank{t}") for t in (0, 1)]
+        for z0 in (0, HALF // 2):
+            gate_and_scale(z, PACK - 1, HALF + z0, HALF // 2, z0)
+            z_q.append((HALF + z0, HALF // 2, weave_and_quantise(z, f"zq1_{z0}", z0, HALF // 2)))
+            for t in (0, 1):
+                product(tail_ps[t][:, z0 : z0 + HALF // 2], low_q, t, z_q[-1][2][0][:], z_q[-1][2][1][:])
+        nc.scalar.copy(h[0][:, cols(1)], tail_ps[0][:])
+        nc.vector.tensor_copy(h[1][:, cols(1)], tail_ps[1][:])
+
+        w2_high = new([P, 2 * N], BF16, "w2_high", "st3")
+        for m0 in (0, 64):
+            dst, src = [view[:, m0 : m0 + 64] for view in pair_views(w2_high, w2_raw, 1)]
+            nc.scalar.copy(dst, src)
+        high_q = quantise(w2_high[:], "w2_high", N // 2, "zq1_128_woven")
+        for t in (2, 3):
+            for c0, width, codes in z_q:
+                product(h_ps[t][:, c0 : c0 + width], high_q, t - 2, codes[0][:], codes[1][:])
+            if t in ():
+                nc.vector.tensor_copy(h[t][:], h_ps[t][:])
+            else:
+                nc.scalar.copy(h[t][:], h_ps[t][:])
 
         out_rows = out.rearrange("(p t) n -> p t n", t=PACK)
         for t in tiles:
-            if t in (1,3):
-                nc.vector.tensor_copy(h[t][:, c], tail_ps[t][:, c])
-            else:
-                nc.scalar.copy(h[t][:, c], tail_ps[t][:, c])
-        for t in tiles:
             a = new([P, S], F32, f"a{t}")
-            b = new([P, S], F32, f"b{t}")
+            b = new([P, S], F32, f"b{t % 2}")
             low = new([P, S], F32, f"low{t}")
             res = new([P, S], F32, f"res{t}")
             for u in halves:
                 gather((t, u) in (), a[:, cols(u)], h[t], "n3", u)
-                gather((t, u) not in ((1,1),(2,1),(3,1)), b[:, cols(u)], h[t], "n4", u)
+                gather((t, u) not in ((3,1),), b[:, cols(u)], h[t], "n4", u)
             pieces = [cols(0), cols(1)] if t == PACK - 1 else [slice(0, S)]
             for c in pieces:
                 nc.vector.tensor_tensor(low[:, c], a[:, c], b[:, c], ALU.min)
             for c in pieces:
-                nc.vector.tensor_tensor(res[:, c], h[t][:, c], low[:, c], ALU.subtract)
+                if t in (0,1):
+                    nc.gpsimd.tensor_tensor(res[:, c], h[t][:, c], low[:, c], ALU.subtract)
+                else:
+                    nc.vector.tensor_tensor(res[:, c], h[t][:, c], low[:, c], ALU.subtract)
                 nc.sync.dma_start(out_rows[:, t, c], res[:, c])

@@ -17,35 +17,69 @@ ACT = mybir.ActivationFunctionType
 
 P = 128
 PACK = 4
+GROUP = 16
+QUADRANT = 32
 HALF = S // 2
-LC = HALF // 16
-PIECES = [(0, 256), (256, 256)]
+QUARTER = S // 4
+TILES = range(PACK)
+FIRST_PAIR, SECOND_PAIR = (0, 1), (2, 3)
+LAST = PACK - 1
+WHOLE = slice(0, S)
+HALVES = (slice(0, HALF), slice(HALF, S))
+LAST_QUARTERS = (slice(HALF, HALF + QUARTER), slice(HALF + QUARTER, S))
 
 
 def tile_picked_layhopdunder_none_p_kernel(
     tc, x_words, x_scales, w1, gn, w2, offs, n1, n2, n3, n4, out
 ):
     nc = tc.nc
-    halves = range(2)
-    tiles = range(PACK)
-
-    def cols(u):
-        return slice(u * HALF, (u + 1) * HALF)
-
-    def entries(lst, u):
-        return lst[:, u * LC : (u + 1) * LC]
 
     with ExitStack() as ctx:
         sb = ctx.enter_context(tc.tile_pool(name="sb", bufs=1))
         ps = ctx.enter_context(tc.psum_pool(name="ps", bufs=1))
 
-        def new(shape, dtype, name, tag=None):
-            return sb.tile(shape, dtype, name=name, tag=tag or name, align_bytes=64)
+        def new(shape, dtype, name, reuses=None):
+            return sb.tile(shape, dtype, name=name, tag=reuses or name, align_bytes=64)
+
+        def new_window(name):
+            return new([P, 2 * S], F32, name)
+
+        def looked_up(window, name, c):
+            return window.indirect(lists[name][:, c.start // GROUP : c.stop // GROUP])
+
+        def gather(on_vector, dst, window, name, c):
+            if on_vector:
+                nc.vector.tensor_copy(dst[:, c], looked_up(window[:], name, c))
+            else:
+                nc.scalar.activation(dst[:, c], looked_up(window[:], name, c), ACT.Copy)
+
+        def pair_views(dealt, raw, pair):
+            dst = dealt[:].rearrange("p (t m j) -> p m j t", t=len(pair), j=PACK)
+            src = raw[:].rearrange("p j (m t) -> p m j t", t=PACK)[:, :, :, pair[0] : pair[-1] + 1]
+            return dst, src
+
+        def quantise(values, name, width, reuses=None):
+            codes = new([P, width], U32, name + "_codes", reuses)
+            scales = new([P, width], U8, name + "_scales")
+            nc.vector.quantize_mx(out=codes[:].bitcast(FP8X4), scales=scales[:], in_=values[:])
+            return codes, scales
+
+        def product(bank, weights, t, codes, scales):
+            m = slice(t % 2 * P, (t % 2 + 1) * P)
+            nc.tensor.matmul_mx(
+                out=bank,
+                lhsT=weights[0][:, m].bitcast(FP8X4),
+                lhsT_scale=weights[1][:, m],
+                rhs=codes.bitcast(FP8X4),
+                rhs_scale=scales,
+                start=True,
+                stop=True,
+            )
 
         lists = {}
         for name in ("offs", "n1", "n2", "n3", "n4"):
-            lists[name] = new([P, S // 16], U16, name)
-        w1_raw = new([P, PACK, H], F32, "w_raw")
+            lists[name] = new([P, S // GROUP], U16, name)
+        w1_raw = new([P, PACK, H], F32, "w1_raw")
         xw = new([P, T], I32, "xw")
         xs = new([P, T], U8, "xs")
         gain = new([P, PACK], F32, "gain")
@@ -58,33 +92,10 @@ def tile_picked_layhopdunder_none_p_kernel(
         nc.sync.dma_start(xw[:], x_words[0].rearrange("p n t -> p (n t)").bitcast(I32))
         nc.sync.dma_start(lists["n4"][:], n4)
         nc.sync.dma_start(gain[:], gn.rearrange("(p t) o -> p (t o)", t=PACK))
-        for q in range(4):
+        for q in range(P // QUADRANT):
             nc.scalar.dma_start(
-                xs_words[32 * q : 32 * q + 4, :],
+                xs_words[QUADRANT * q : QUADRANT * q + 4, :],
                 x_scales[0, 4 * q : 4 * q + 4, :].bitcast(I32),
-            )
-
-        def pair_views(dealt, raw, pair):
-            dst = dealt[:].rearrange("p (t m j) -> p m j t", t=2, j=PACK)
-            src = raw[:].rearrange("p j (m t) -> p m j t", t=PACK)[:, :, :, 2 * pair : 2 * pair + 2]
-            return dst, src
-
-        def quantise(values, name, width, codes_tag=None):
-            codes = new([P, width], U32, name + "_codes", codes_tag)
-            scales = new([P, width], U8, name + "_scales")
-            nc.vector.quantize_mx(out=codes[:].bitcast(FP8X4), scales=scales[:], in_=values)
-            return codes, scales
-
-        def product(bank, w, t, moving_codes, moving_scales):
-            m = slice(t * P, (t + 1) * P)
-            nc.tensor.matmul_mx(
-                out=bank,
-                lhsT=w[0][:, m].bitcast(FP8X4),
-                lhsT_scale=w[1][:, m],
-                rhs=moving_codes.bitcast(FP8X4),
-                rhs_scale=moving_scales,
-                start=True,
-                stop=True,
             )
 
         warm_in = new([P, 1], F32, "warm_in")
@@ -92,119 +103,111 @@ def tile_picked_layhopdunder_none_p_kernel(
         nc.vector.memset(warm_in[:], 0.0)
         nc.scalar.activation(warm_out[:], warm_in[:], ACT.Sigmoid)
 
-        xs_g = new([P, S], U8, "xs_g")
-        nc.vector.tensor_copy(xs_g[:], xs[:].indirect(lists["offs"][:]))
-        w1_bf = [new([P, 2 * H], BF16, f"w1_bf{pair}") for pair in range(2)]
-        for pair in range(2):
-            nc.scalar.copy(*pair_views(w1_bf[pair], w1_raw, pair))
-        w2_raw = new([P, PACK, N], F32, "w_raw")
+        xs_picked = new([P, S], U8, "xs_picked")
+        nc.vector.tensor_copy(xs_picked[:], looked_up(xs[:], "offs", WHOLE))
+        w1_first = new([P, 2 * H], BF16, "w1_first")
+        w1_second = new([P, 2 * H], BF16, "w1_second")
+        nc.scalar.copy(*pair_views(w1_first, w1_raw, FIRST_PAIR))
+        nc.scalar.copy(*pair_views(w1_second, w1_raw, SECOND_PAIR))
+        w2_raw = new([P, PACK, N], F32, "w2_raw", reuses="w1_raw")
         nc.sync.dma_start(w2_raw[:], w2.rearrange("(p j) c -> p j c", j=PACK))
 
-        y_ps = [ps.tile([P, S], F32, name=f"y_ps{t}", tag=f"low_bank{t}") for t in tiles]
-        w1_low_q = quantise(w1_bf[0][:], "w1_low", H // 2, "xs")
-        xw_g = new([P, S], U32, "xw_g", "w1_bf0")
-        for u in halves:
-            nc.vector.tensor_copy(xw_g[:, cols(u)], xw[:].bitcast(U32).indirect(entries(lists["offs"], u)))
-        for u in halves:
-            for t in (0, 1):
-                product(y_ps[t][:, cols(u)], w1_low_q, t, xw_g[:, cols(u)], xs_g[:, cols(u)])
-        w1_high_q = quantise(w1_bf[1][:], "w1_high", H // 2, "xw")
-        for t in (2, 3):
-            product(y_ps[t][:], w1_high_q, t - 2, xw_g[:], xs_g[:])
+        y_ps = [ps.tile([P, S], F32, name=f"y_ps{t}", tag=f"y_bank{t}") for t in TILES]
+        w1_first_q = quantise(w1_first, "w1_first", H // 2, reuses="xs")
+        xw_picked = new([P, S], U32, "xw_picked", reuses="w1_first")
+        for c in HALVES:
+            nc.vector.tensor_copy(xw_picked[:, c], looked_up(xw[:].bitcast(U32), "offs", c))
+        for c in HALVES:
+            for t in FIRST_PAIR:
+                product(y_ps[t][:, c], w1_first_q, t, xw_picked[:, c], xs_picked[:, c])
+        w1_second_q = quantise(w1_second, "w1_second", H // 2, reuses="xw")
+        for t in SECOND_PAIR:
+            product(y_ps[t][:], w1_second_q, t, xw_picked[:], xs_picked[:])
 
-        def gather(on_vector, dst_ap, window, lst, u):
-            looked_up = window[:].indirect(entries(lists[lst], u))
-            if on_vector:
-                nc.vector.tensor_copy(dst_ap, looked_up)
-            else:
-                nc.scalar.activation(dst_ap, looked_up, ACT.Copy)
-
-        y = [new([P, S], F32, f"y{t}") for t in tiles]
-        hop = [new([P, S], F32, f"hop{t}") for t in tiles]
-        st = [new([P, S], F32, f"st{t}") for t in tiles]
-        for t in tiles:
-            if t in (0,):
-                nc.vector.tensor_copy(y[t][:], y_ps[t][:])
-            else:
-                nc.scalar.copy(y[t][:], y_ps[t][:])
-        for t in tiles:
-            for u in halves:
-                gather((t, u) not in ((1, 0), (1, 1), (3, 0), (3, 1)), hop[t][:, cols(u)], y[t], "n1", u)
-        for t in tiles:
+        y = [new_window(f"y{t}") for t in TILES]
+        hop = [new([P, S], F32, f"hop{t}") for t in TILES]
+        st = [new([P, S], F32, f"st{t}") for t in TILES]
+        nc.vector.tensor_copy(y[0][:, WHOLE], y_ps[0][:])
+        for t in TILES[1:]:
+            nc.scalar.copy(y[t][:, WHOLE], y_ps[t][:])
+        for t in TILES:
+            gather(t % 2 == 0, hop[t], y[t], "n1", WHOLE)
+        for t in TILES:
             nc.vector.tensor_tensor(st[t][:], hop[t][:], y_ps[t][:], ALU.subtract)
 
-        h_ps = [ps.tile([P, S], F32, name=f"h_ps{t}", tag=f"high_bank{t}") for t in tiles]
-        h = [new([P, S], F32, f"h{t}") for t in tiles]
-        gates = [new([P, HALF], F32, f"gate{r}") for r in tiles]
-        def gate_and_scale(z, t, c0, width, z0):
-            looked_up = st[t][:].indirect(lists["n2"][:, c0 // 16 : (c0 + width) // 16])
-            gate = gates[t][:, z0 : z0 + width]
-            nc.scalar.activation(gate, looked_up, ACT.Sigmoid)
+        gates = [new([P, HALF], F32, f"gate{t}") for t in TILES]
+
+        def gate_and_scale(z, t, c):
+            in_half = slice(c.start % HALF, c.start % HALF + c.stop - c.start)
+            nc.scalar.activation(gates[t][:, in_half], looked_up(st[t][:], "n2", c), ACT.Sigmoid)
             nc.vector.scalar_tensor_tensor(
-                z[:, t, z0 : z0 + width], y_ps[t][:, c0 : c0 + width], gain[:, t : t + 1], gate, ALU.mult, ALU.mult
+                z[:, t, in_half], y_ps[t][:, c], gain[:, t : t + 1], gates[t][:, in_half], ALU.mult, ALU.mult
             )
 
-        def weave_and_quantise(z, name, z0, width):
-            zi = new([P, PACK * width], BF16, name + "_woven")
+        def weave_and_quantise(z, c):
+            width = c.stop - c.start
+            woven = new([P, PACK * width], BF16, f"woven{c.start}")
             nc.vector.tensor_copy(
-                zi[:].rearrange("p (c i t) -> p c t i", i=4, t=PACK),
-                z[:, :, z0 : z0 + width].rearrange("p t (c i) -> p c t i", i=4),
+                woven[:].rearrange("p (c i t) -> p c t i", i=4, t=PACK),
+                z[:, :, c.start % HALF : c.start % HALF + width].rearrange("p t (c i) -> p c t i", i=4),
             )
-            return quantise(zi[:], name, width)
+            return quantise(woven, f"z{c.start}", width)
 
+        h_ps = [ps.tile([P, S], F32, name=f"h_ps{t}", tag=f"h_bank{t}") for t in TILES]
+        h = [new_window(f"h{t}") for t in TILES]
         z_q = []
-        z = new([P, PACK, HALF], BF16, "z0")
-        for t in tiles:
-            gate_and_scale(z, t, 0, HALF, 0)
-        w2_low = new([P, 2 * N], BF16, "w2_low")
-        for t in (0, 1):
-            dst, src = [view[:, :, :, t] for view in pair_views(w2_low, w2_raw, 0)]
-            nc.gpsimd.tensor_scalar(dst, src, 1.0, 0.0, ALU.mult, ALU.add)
-        low_q = quantise(w2_low[:], "w2_low", N // 2)
-        z_q.append((0, HALF, weave_and_quantise(z, "zq0", 0, HALF)))
-        for t in (0, 1):
-            product(h_ps[t][:, cols(0)], low_q, t, z_q[0][2][0][:], z_q[0][2][1][:])
-            nc.scalar.copy(h[t][:, cols(0)], h_ps[t][:, cols(0)])
-        z = new([P, PACK, HALF], BF16, "z1")
-        for t in range(PACK - 1):
-            gate_and_scale(z, t, HALF, HALF, 0)
-        tail_ps = [ps.tile([P, HALF], F32, name=f"tail_ps{t}", tag=f"low_bank{t}") for t in (0, 1)]
-        for z0 in (0, HALF // 2):
-            gate_and_scale(z, PACK - 1, HALF + z0, HALF // 2, z0)
-            z_q.append((HALF + z0, HALF // 2, weave_and_quantise(z, f"zq1_{z0}", z0, HALF // 2)))
-            for t in (0, 1):
-                product(tail_ps[t][:, z0 : z0 + HALF // 2], low_q, t, z_q[-1][2][0][:], z_q[-1][2][1][:])
-        nc.scalar.copy(h[0][:, cols(1)], tail_ps[0][:])
-        nc.vector.tensor_copy(h[1][:, cols(1)], tail_ps[1][:])
 
-        w2_high = new([P, 2 * N], BF16, "w2_high", "st3")
-        for m0 in (0, 64):
-            dst, src = [view[:, m0 : m0 + 64] for view in pair_views(w2_high, w2_raw, 1)]
-            nc.scalar.copy(dst, src)
-        high_q = quantise(w2_high[:], "w2_high", N // 2, "zq1_128_woven")
-        for t in (2, 3):
-            for c0, width, codes in z_q:
-                product(h_ps[t][:, c0 : c0 + width], high_q, t - 2, codes[0][:], codes[1][:])
-            if t in ():
-                nc.vector.tensor_copy(h[t][:], h_ps[t][:])
-            else:
-                nc.scalar.copy(h[t][:], h_ps[t][:])
+        z_left = new([P, PACK, HALF], BF16, "z_left")
+        for t in TILES:
+            gate_and_scale(z_left, t, HALVES[0])
+        w2_first = new([P, 2 * N], BF16, "w2_first", reuses="y2")
+        dst, src = pair_views(w2_first, w2_raw, FIRST_PAIR)
+        for t in FIRST_PAIR:
+            nc.gpsimd.tensor_scalar(dst[:, :, :, t], src[:, :, :, t], 1.0, 0.0, ALU.mult, ALU.add)
+        w2_first_q = quantise(w2_first, "w2_first", N // 2)
+        z_q.append((HALVES[0], *weave_and_quantise(z_left, HALVES[0])))
+        for t in FIRST_PAIR:
+            product(h_ps[t][:, HALVES[0]], w2_first_q, t, z_q[0][1][:], z_q[0][2][:])
+            nc.scalar.copy(h[t][:, HALVES[0]], h_ps[t][:, HALVES[0]])
+
+        z_right = new([P, PACK, HALF], BF16, "z_right")
+        for t in TILES[:LAST]:
+            gate_and_scale(z_right, t, HALVES[1])
+        right_ps = [ps.tile([P, HALF], F32, name=f"right_ps{t}", tag=f"y_bank{t}") for t in FIRST_PAIR]
+        for c in LAST_QUARTERS:
+            gate_and_scale(z_right, LAST, c)
+            z_q.append((c, *weave_and_quantise(z_right, c)))
+            for t in FIRST_PAIR:
+                product(right_ps[t][:, c.start - HALF : c.stop - HALF], w2_first_q, t, z_q[-1][1][:], z_q[-1][2][:])
+        nc.scalar.copy(h[0][:, HALVES[1]], right_ps[0][:])
+        nc.vector.tensor_copy(h[1][:, HALVES[1]], right_ps[1][:])
+
+        w2_second = new([P, 2 * N], BF16, "w2_second", reuses=f"st{LAST}")
+        dst, src = pair_views(w2_second, w2_raw, SECOND_PAIR)
+        for m0 in (0, P // 2):
+            nc.scalar.copy(dst[:, m0 : m0 + P // 2], src[:, m0 : m0 + P // 2])
+        w2_second_q = quantise(w2_second, "w2_second", N // 2, reuses=f"woven{LAST_QUARTERS[-1].start}")
+        for t in SECOND_PAIR:
+            for c, codes, scales in z_q:
+                product(h_ps[t][:, c], w2_second_q, t, codes[:], scales[:])
+            nc.scalar.copy(h[t][:, WHOLE], h_ps[t][:])
 
         out_rows = out.rearrange("(p t) n -> p t n", t=PACK)
-        for t in tiles:
-            a = new([P, S], F32, f"a{t}")
-            b = new([P, S], F32, f"b{t % 2}")
+        for t in TILES:
+            at_n3 = new([P, S], F32, f"at_n3_{t}")
+            at_n4 = new([P, S], F32, f"at_n4_{t}")
             low = new([P, S], F32, f"low{t}")
             res = new([P, S], F32, f"res{t}")
-            for u in halves:
-                gather((t, u) in (), a[:, cols(u)], h[t], "n3", u)
-                gather((t, u) not in ((3,1),), b[:, cols(u)], h[t], "n4", u)
-            pieces = [cols(0), cols(1)] if t == PACK - 1 else [slice(0, S)]
+            pieces = HALVES if t == LAST else (WHOLE,)
             for c in pieces:
-                nc.vector.tensor_tensor(low[:, c], a[:, c], b[:, c], ALU.min)
+                gather(False, at_n3, h[t], "n3", c)
+            if t in FIRST_PAIR:
+                gather(True, at_n4, h[t], "n4", WHOLE)
+            else:
+                gather(True, at_n4, h[t], "n4", HALVES[0])
+                gather(False, at_n4, h[t], "n4", HALVES[1])
             for c in pieces:
-                if t in (0,1):
-                    nc.gpsimd.tensor_tensor(res[:, c], h[t][:, c], low[:, c], ALU.subtract)
-                else:
-                    nc.vector.tensor_tensor(res[:, c], h[t][:, c], low[:, c], ALU.subtract)
+                nc.vector.tensor_tensor(low[:, c], at_n3[:, c], at_n4[:, c], ALU.min)
+            for c in pieces:
+                nc.vector.tensor_tensor(res[:, c], h[t][:, c], low[:, c], ALU.subtract)
                 nc.sync.dma_start(out_rows[:, t, c], res[:, c])

from contextlib import ExitStack

import concourse.mybir as mybir

K, T, S, N, H = 512, 2048, 512, 512, 512
FLOPS = 2 * K * H * S + 2 * H * N * S

F32 = mybir.dt.float32
BF16 = mybir.dt.bfloat16
I32 = mybir.dt.int32
U32 = mybir.dt.uint32
U16 = mybir.dt.uint16
U8 = mybir.dt.uint8
FP8X4 = mybir.dt.float8_e4m3fn_x4
ALU = mybir.AluOpType
ACT = mybir.ActivationFunctionType

P = 128
PACK = 4
GROUP = 16
QUADRANT = 32
HALF = S // 2
QUARTER = S // 4
TILES = range(PACK)
FIRST_PAIR, SECOND_PAIR = (0, 1), (2, 3)
LAST = PACK - 1
WHOLE = slice(0, S)
HALVES = (slice(0, HALF), slice(HALF, S))
LAST_QUARTERS = (slice(HALF, HALF + QUARTER), slice(HALF + QUARTER, S))


def tile_picked_layhopdunder_none_p_kernel(
    tc, x_words, x_scales, w1, gn, w2, offs, n1, n2, n3, n4, out
):
    nc = tc.nc

    with ExitStack() as ctx:
        sb = ctx.enter_context(tc.tile_pool(name="sb", bufs=1))
        ps = ctx.enter_context(tc.psum_pool(name="ps", bufs=1))

        def new(shape, dtype, name, reuses=None):
            return sb.tile(shape, dtype, name=name, tag=reuses or name, align_bytes=64)

        def new_window(name):
            return new([P, 2 * S], F32, name)

        def looked_up(window, name, c):
            return window.indirect(lists[name][:, c.start // GROUP : c.stop // GROUP])

        def gather(on_vector, dst, window, name, c):
            if on_vector:
                nc.vector.tensor_copy(dst[:, c], looked_up(window[:], name, c))
            else:
                nc.scalar.activation(dst[:, c], looked_up(window[:], name, c), ACT.Copy)

        def pair_views(dealt, raw, pair):
            dst = dealt[:].rearrange("p (t m j) -> p m j t", t=len(pair), j=PACK)
            src = raw[:].rearrange("p j (m t) -> p m j t", t=PACK)[:, :, :, pair[0] : pair[-1] + 1]
            return dst, src

        def quantise(values, name, width, reuses=None):
            codes = new([P, width], U32, name + "_codes", reuses)
            scales = new([P, width], U8, name + "_scales")
            nc.vector.quantize_mx(out=codes[:].bitcast(FP8X4), scales=scales[:], in_=values[:])
            return codes, scales

        def product(bank, weights, t, codes, scales):
            m = slice(t % 2 * P, (t % 2 + 1) * P)
            nc.tensor.matmul_mx(
                out=bank,
                lhsT=weights[0][:, m].bitcast(FP8X4),
                lhsT_scale=weights[1][:, m],
                rhs=codes.bitcast(FP8X4),
                rhs_scale=scales,
                start=True,
                stop=True,
            )

        lists = {}
        for name in ("offs", "n1", "n2", "n3", "n4"):
            lists[name] = new([P, S // GROUP], U16, name)
        w1_raw = new([P, PACK, H], F32, "w1_raw")
        xw = new([P, T], I32, "xw")
        xs = new([P, T], U8, "xs")
        gain = new([P, PACK], F32, "gain")

        xs_words = xs[:].bitcast(I32)
        nc.vector.memset(xs_words, 0)
        for name, source in (("offs", offs), ("n1", n1), ("n2", n2), ("n3", n3)):
            nc.sync.dma_start(lists[name][:], source)
        nc.sync.dma_start(w1_raw[:], w1.rearrange("(p j) c -> p j c", j=PACK))
        nc.sync.dma_start(xw[:], x_words[0].rearrange("p n t -> p (n t)").bitcast(I32))
        nc.sync.dma_start(lists["n4"][:], n4)
        nc.sync.dma_start(gain[:], gn.rearrange("(p t) o -> p (t o)", t=PACK))
        for q in range(P // QUADRANT):
            nc.scalar.dma_start(
                xs_words[QUADRANT * q : QUADRANT * q + 4, :],
                x_scales[0, 4 * q : 4 * q + 4, :].bitcast(I32),
            )

        warm_in = new([P, 1], F32, "warm_in")
        warm_out = new([P, 1], F32, "warm_out")
        nc.vector.memset(warm_in[:], 0.0)
        nc.scalar.activation(warm_out[:], warm_in[:], ACT.Sigmoid)

        xs_picked = new([P, S], U8, "xs_picked")
        nc.vector.tensor_copy(xs_picked[:], looked_up(xs[:], "offs", WHOLE))
        w1_first = new([P, 2 * H], BF16, "w1_first")
        w1_second = new([P, 2 * H], BF16, "w1_second")
        nc.scalar.copy(*pair_views(w1_first, w1_raw, FIRST_PAIR))
        nc.scalar.copy(*pair_views(w1_second, w1_raw, SECOND_PAIR))
        w2_raw = new([P, PACK, N], F32, "w2_raw", reuses="w1_raw")
        nc.sync.dma_start(w2_raw[:], w2.rearrange("(p j) c -> p j c", j=PACK))

        y_ps = [ps.tile([P, S], F32, name=f"y_ps{t}", tag=f"y_bank{t}") for t in TILES]
        w1_first_q = quantise(w1_first, "w1_first", H // 2, reuses="xs")
        xw_picked = new([P, S], U32, "xw_picked", reuses="w1_first")
        for c in HALVES:
            nc.vector.tensor_copy(xw_picked[:, c], looked_up(xw[:].bitcast(U32), "offs", c))
        for c in HALVES:
            for t in FIRST_PAIR:
                product(y_ps[t][:, c], w1_first_q, t, xw_picked[:, c], xs_picked[:, c])
        w1_second_q = quantise(w1_second, "w1_second", H // 2, reuses="xw")
        for t in SECOND_PAIR:
            product(y_ps[t][:], w1_second_q, t, xw_picked[:], xs_picked[:])

        y = [new_window(f"y{t}") for t in TILES]
        hop = [new([P, S], F32, f"hop{t}") for t in TILES]
        st = [new([P, S], F32, f"st{t}") for t in TILES]
        nc.vector.tensor_copy(y[0][:, WHOLE], y_ps[0][:])
        for t in TILES[1:]:
            nc.scalar.copy(y[t][:, WHOLE], y_ps[t][:])
        for t in TILES:
            gather(t % 2 == 0, hop[t], y[t], "n1", WHOLE)
        for t in TILES:
            nc.vector.tensor_tensor(st[t][:], hop[t][:], y_ps[t][:], ALU.subtract)

        gates = [new([P, HALF], F32, f"gate{t}") for t in TILES]

        def gate_and_scale(z, t, c):
            in_half = slice(c.start % HALF, c.start % HALF + c.stop - c.start)
            nc.scalar.activation(gates[t][:, in_half], looked_up(st[t][:], "n2", c), ACT.Sigmoid)
            nc.vector.scalar_tensor_tensor(
                z[:, t, in_half], y_ps[t][:, c], gain[:, t : t + 1], gates[t][:, in_half], ALU.mult, ALU.mult
            )

        def weave_and_quantise(z, c):
            width = c.stop - c.start
            woven = new([P, PACK * width], BF16, f"woven{c.start}")
            nc.vector.tensor_copy(
                woven[:].rearrange("p (c i t) -> p c t i", i=4, t=PACK),
                z[:, :, c.start % HALF : c.start % HALF + width].rearrange("p t (c i) -> p c t i", i=4),
            )
            return quantise(woven, f"z{c.start}", width)

        h_ps = [ps.tile([P, S], F32, name=f"h_ps{t}", tag=f"h_bank{t}") for t in TILES]
        h = [new_window(f"h{t}") for t in TILES]
        z_q = []

        z_left = new([P, PACK, HALF], BF16, "z_left")
        for t in TILES:
            gate_and_scale(z_left, t, HALVES[0])
        w2_first = new([P, 2 * N], BF16, "w2_first", reuses="y2")
        dst, src = pair_views(w2_first, w2_raw, FIRST_PAIR)
        for t in FIRST_PAIR:
            nc.gpsimd.tensor_scalar(dst[:, :, :, t], src[:, :, :, t], 1.0, 0.0, ALU.mult, ALU.add)
        w2_first_q = quantise(w2_first, "w2_first", N // 2)
        z_q.append((HALVES[0], *weave_and_quantise(z_left, HALVES[0])))
        for t in FIRST_PAIR:
            product(h_ps[t][:, HALVES[0]], w2_first_q, t, z_q[0][1][:], z_q[0][2][:])
            nc.scalar.copy(h[t][:, HALVES[0]], h_ps[t][:, HALVES[0]])

        z_right = new([P, PACK, HALF], BF16, "z_right")
        for t in TILES[:LAST]:
            gate_and_scale(z_right, t, HALVES[1])
        right_ps = [ps.tile([P, HALF], F32, name=f"right_ps{t}", tag=f"y_bank{t}") for t in FIRST_PAIR]
        for c in LAST_QUARTERS:
            gate_and_scale(z_right, LAST, c)
            z_q.append((c, *weave_and_quantise(z_right, c)))
            for t in FIRST_PAIR:
                product(right_ps[t][:, c.start - HALF : c.stop - HALF], w2_first_q, t, z_q[-1][1][:], z_q[-1][2][:])
        nc.scalar.copy(h[0][:, HALVES[1]], right_ps[0][:])
        nc.vector.tensor_copy(h[1][:, HALVES[1]], right_ps[1][:])

        w2_second = new([P, 2 * N], BF16, "w2_second", reuses=f"st{LAST}")
        dst, src = pair_views(w2_second, w2_raw, SECOND_PAIR)
        for m0 in (0, P // 2):
            nc.scalar.copy(dst[:, m0 : m0 + P // 2], src[:, m0 : m0 + P // 2])
        w2_second_q = quantise(w2_second, "w2_second", N // 2, reuses=f"woven{LAST_QUARTERS[-1].start}")
        for t in SECOND_PAIR:
            for c, codes, scales in z_q:
                product(h_ps[t][:, c], w2_second_q, t, codes[:], scales[:])
            nc.scalar.copy(h[t][:, WHOLE], h_ps[t][:])

        out_rows = out.rearrange("(p t) n -> p t n", t=PACK)
        for t in TILES:
            at_n3 = new([P, S], F32, f"at_n3_{t}")
            at_n4 = new([P, S], F32, f"at_n4_{t}")
            low = new([P, S], F32, f"low{t}")
            res = new([P, S], F32, f"res{t}")
            pieces = HALVES if t == LAST else (WHOLE,)
            for c in pieces:
                gather(False, at_n3, h[t], "n3", c)
            if t in FIRST_PAIR:
                gather(True, at_n4, h[t], "n4", WHOLE)
            else:
                gather(True, at_n4, h[t], "n4", HALVES[0])
                gather(False, at_n4, h[t], "n4", HALVES[1])
            for c in pieces:
                nc.vector.tensor_tensor(low[:, c], at_n3[:, c], at_n4[:, c], ALU.min)
            for c in pieces:
                nc.vector.tensor_tensor(res[:, c], h[t][:, c], low[:, c], ALU.subtract)
                nc.sync.dma_start(out_rows[:, t, c], res[:, c])
